import numpy as np
import ml_dtypes


def mxq(x, axis, fmt="e4m3"):
    dtype, down = {"e4m3": (ml_dtypes.float8_e4m3fn, 7), "e5m2": (ml_dtypes.float8_e5m2, 14)}[fmt]
    v = np.moveaxis(np.asarray(x, np.float32).astype(ml_dtypes.bfloat16).astype(np.float64), axis, -1)
    blocks = v.reshape(v.shape[:-1] + (-1, 32))
    amax = np.abs(blocks).max(-1, keepdims=True)
    byte = np.maximum(np.where(amax > 0, np.frexp(amax)[1] - 1 + 127, 0) - down, 1)
    scale = np.exp2(byte - 127.0)
    codes = (blocks / scale).astype(np.float32).astype(dtype).astype(np.float64)
    return np.moveaxis((codes * scale).reshape(v.shape), -1, axis)


WIDE = False


def mx_kscale(k):
    if not WIDE:
        return np.ones(k)
    levels = np.array([30, -30])
    if k % 512:
        return np.exp2(np.random.permutation(np.resize(levels, k // 32))).repeat(32)
    a = np.empty((k // 512, 16))
    for p in range(k // 512):
        a[p, :8] = np.random.permutation(np.resize(levels, 8))
        for g in range(8):
            far = levels[np.abs(levels - a[p, g]) >= 10]
            a[p, g + 8] = far[np.random.randint(len(far))]
    return np.exp2(a.ravel()).repeat(32)


def f64(x):
    return np.asarray(x).astype(np.float64)


def striped(idx):
    return np.tile(np.asarray(idx).reshape(-1, 16).T, (8, 1)).astype(np.uint16)


def unstriped(offs):
    return offs[:16].T.reshape(-1).astype(np.int64)


E2M1 = np.array([0.0, 0.5, 1.0, 1.5, 2.0, 3.0, 4.0, 6.0, -0.0, -0.5, -1.0, -1.5, -2.0, -3.0, -4.0, -6.0])


def pack_weight(w, fmt):
    k, n = w.shape
    w = f64(np.asarray(w, np.float32).astype(ml_dtypes.bfloat16)).reshape(k // 32, 32, n)
    amax = np.abs(w).max(1)
    if fmt == "e4m3":
        byte = np.frexp(amax)[1] - 1 + 127 - 7
    else:
        mant, ex = np.frexp(amax / 6.0)
        byte = np.where(mant > 0.5, ex, ex - 1) + 127
    byte = np.clip(np.where(amax > 0, byte, 1), 1, 254)
    scaled = (w * np.exp2(127.0 - byte)[:, None, :]).reshape(k, n).astype(np.float32)
    by_word = np.ascontiguousarray(scaled.reshape(k // 512, 128, 4, n).transpose(0, 1, 3, 2))
    if fmt == "e4m3":
        words = by_word.astype(ml_dtypes.float8_e4m3fn).view(np.uint8)
    else:
        c = by_word.astype(ml_dtypes.float4_e2m1fn).view(np.uint8) & 0xF
        words = (c[..., 0::2] | (c[..., 1::2] << 4)).reshape(k // 512, 128, 2 * n)
    return np.ascontiguousarray(words), np.ascontiguousarray(byte.astype(np.uint8).reshape(k // 512, 16, n))


def unpack_weight(words, scales, fmt):
    g, _, n = scales.shape
    words = np.ascontiguousarray(words).reshape(g, 128, n, -1)
    if fmt == "e4m3":
        vals = words.view(ml_dtypes.float8_e4m3fn).astype(np.float64)
    else:
        nib = np.empty((g, 128, n, 4), np.uint8)
        nib[..., 0::2] = words & 0xF
        nib[..., 1::2] = words >> 4
        vals = E2M1[nib]
    vals = vals * np.repeat(np.exp2(scales.astype(np.float64) - 127.0), 8, axis=1)[..., None]
    return vals.transpose(0, 1, 3, 2).reshape(g * 512, n)


K, T, J, I, V, G = 1024, 1024, 256, 256, 1024, 32


def setup_inputs():
    n = np.random.standard_normal
    idx = np.random.permutation(T)[:J]
    idx2 = np.random.permutation(T)[:J]
    idx3 = np.random.permutation(V)[:I]
    fk = mx_kscale(K)
    kyp = pack_weight(n((K, V)) / fk[:, None], "e2m1")
    return {
        "xf": (n((K, T)) * 0.03).astype(np.float32),
        "fk": (np.random.uniform(0.5, 2.0, (K, 1)) * fk[:, None]).astype(np.float32),
        "ky_words": kyp[0],
        "ky_scales": kyp[1],
        "bi": (np.random.uniform(-0.7, 0.7, (1, I))).astype(np.float32),
        "offs": striped(idx),
        "offs2": striped(idx2),
        "offs3": striped(idx3),
    }


def reference(xf, fk, ky_words, ky_scales, bi, offs, offs2, offs3):
    idx = unstriped(offs)
    idx2 = unstriped(offs2)
    idx3 = unstriped(offs3)
    kyu = unpack_weight(ky_words, ky_scales, "e2m1")
    u = (f64(xf)[:, idx] - f64(xf)[:, idx2]) * f64(fk)
    uq = mxq(u, 0, "e5m2")
    kyidx3g = kyu[:, idx3]
    a0 = uq.T @ kyidx3g
    a = a0 + f64(bi)
    g1 = a.reshape(J, G, I // G).max(axis=2)
    y = g1 - 0.5 * np.max(a, axis=1, keepdims=True)
    return y

@@ -1,0 +1,149 @@
+from contextlib import ExitStack
+
+import concourse.mybir as mybir
+from concourse.masks import make_identity
+
+K, T, J, I, V, G = 1024, 1024, 256, 256, 1024, 32
+FLOPS = 2 * K * J * I
+
+F32 = mybir.dt.float32
+BF16 = mybir.dt.bfloat16
+I32 = mybir.dt.int32
+U32 = mybir.dt.uint32
+U16 = mybir.dt.uint16
+U8 = mybir.dt.uint8
+E5M2X4 = mybir.dt.float8_e5m2_x4
+E2M1X4 = mybir.dt.float4_e2m1fn_x4
+ALU = mybir.AluOpType
+COPY = mybir.ActivationFunctionType.Copy
+AX = mybir.AxisListType.X
+
+P = 128
+PACK = 4
+PASSES = K // (P * PACK)
+HALVES = J // P
+BUNDLE = I // G
+
+
+def tile_list_scores_gaps_listed_bundles_kernel(tc, xf, fk, ky_words, ky_scales, bi, offs, offs2, offs3, out):
+    nc = tc.nc
+    with ExitStack() as ctx:
+        sb = ctx.enter_context(tc.tile_pool(name="sb", bufs=1))
+        ps = ctx.enter_context(tc.psum_pool(name="ps", bufs=1))
+
+        list1 = sb.tile([P, J // 16], U16, name="list1")
+        list2 = sb.tile([P, J // 16], U16, name="list2")
+        list3 = sb.tile([P, I // 16], U16, name="list3")
+        rows = [sb.tile([P, T], F32, name="rows%d" % n) for n in range(8)]
+        kw = [sb.tile([P, V], U16, name="kw%d" % a) for a in range(PASSES)]
+        ks = sb.tile([P, PASSES * V], U8, name="ks")
+        fac = sb.tile([P, PASSES, PACK], F32, name="fac")
+        bcol = sb.tile([P, 2], F32, name="bcol")
+        ident = sb.tile([P, P], F32, name="ident")
+        bias = sb.tile([P, I], F32, name="bias")
+        xr = xf.rearrange("(a p t) c -> a t p c", a=PASSES, t=PACK)
+
+        def load_rows(n):
+            nc.sync.dma_start(out=rows[n][:], in_=xr[n // PACK, n % PACK])
+
+        def load_words(a):
+            nc.sync.dma_start(out=kw[a][:].bitcast(I32), in_=ky_words[a].bitcast(I32))
+
+        nc.vector.memset(ks[:].bitcast(I32), 0)
+        ksr = ky_scales.bitcast(I32).rearrange("a (q r) v -> r q a v", r=4)
+        make_identity(nc, ident[:])
+
+        load_rows(0)
+        nc.sync.dma_start(out=list2[:], in_=offs2)
+        nc.sync.dma_start(out=list1[:], in_=offs)
+        load_rows(1)
+        nc.sync.dma_start(out=fac[:], in_=fk.rearrange("(a p t) o -> p a (t o)", a=PASSES, t=PACK))
+        nc.sync.dma_start(out=list3[:], in_=offs3)
+        load_rows(2)
+        load_words(0)
+        for r in range(4):
+            nc.sync.dma_start(out=ks[r:P:32, :].bitcast(I32).rearrange("q (a v) -> q a v", a=PASSES), in_=ksr[r])
+        load_rows(3)
+        load_words(1)
+        load_rows(4)
+        nc.sync.dma_start(out=bcol[:], in_=bi.rearrange("o (p c) -> p (o c)", c=2))
+        for n in range(5, 8):
+            load_rows(n)
+
+        second = [sb.tile([P, J], F32, name="second%d" % n) for n in range(8)]
+        first = [sb.tile([P, P], F32, name="first%d" % n) for n in range(8)]
+        gap = [[sb.tile([P, P], F32, name="gap%d_%d" % (n, h)) for h in range(HALVES)] for n in range(8)]
+        u = [[sb.tile([P, P * PACK], BF16, name="u%d_%d" % (a, h), align_bytes=64) for h in range(HALVES)] for a in range(PASSES)]
+        uc = [[sb.tile([P, P], U32, name="uc%d_%d" % (a, h), align_bytes=64) for h in range(HALVES)] for a in range(PASSES)]
+        us = [[sb.tile([P, P], U8, name="us%d_%d" % (a, h), align_bytes=64) for h in range(HALVES)] for a in range(PASSES)]
+        kwg = [sb.tile([P, I], U16, name="kwg%d" % a, align_bytes=64) for a in range(PASSES)]
+        ksg = [sb.tile([P, I], U8, name="ksg%d" % a, align_bytes=64) for a in range(PASSES)]
+        acc = [ps.tile([P, I], F32, name="acc%d" % h) for h in range(HALVES)]
+        bps = ps.tile([P, 2, P], F32, name="bps")
+
+        def half(h):
+            return slice(h * P, (h + 1) * P)
+
+        def entries(lst, h):
+            return lst[:, 8 * h : 8 * h + 8]
+
+        def weave(n, h):
+            a, t = divmod(n, PACK)
+            nc.vector.tensor_scalar(
+                out=u[a][h][:].rearrange("p (j t) -> p j t", t=PACK)[:, :, t],
+                in0=gap[n][h][:], scalar1=fac[:, a, t : t + 1], scalar2=None, op0=ALU.mult)
+
+        def product(a, h):
+            nc.vector.quantize_mx(out=uc[a][h][:].bitcast(E5M2X4), scales=us[a][h][:], in_=u[a][h][:])
+            nc.tensor.matmul_mx(
+                out=acc[h][:], lhsT=uc[a][h][:].bitcast(E5M2X4), lhsT_scale=us[a][h][:],
+                rhs=kwg[a][:].bitcast(E2M1X4), rhs_scale=ksg[a][:], start=(a == 0), stop=(a == PASSES - 1))
+
+        def gaps(n):
+            nc.scalar.activation(out=second[n][:, half(0)], in_=rows[n][:].indirect(entries(list2, 0)), func=COPY)
+            nc.scalar.activation(out=second[n][:, half(1)], in_=rows[n][:].indirect(entries(list2, 1)), func=COPY)
+            nc.scalar.activation(out=first[n][:], in_=rows[n][:].indirect(entries(list1, 1)), func=COPY)
+            nc.vector.tensor_tensor(out=gap[n][0][:], in0=rows[n][:].indirect(entries(list1, 0)),
+                                    in1=second[n][:, half(0)], op=ALU.subtract)
+            weave(n, 0)
+            nc.vector.tensor_tensor(out=gap[n][1][:], in0=first[n][:], in1=second[n][:, half(1)], op=ALU.subtract)
+            weave(n, 1)
+
+        def pick_words(a):
+            nc.vector.tensor_copy(out=kwg[a][:], in_=kw[a][:].indirect(list3[:]))
+
+        def pick_scales(a):
+            nc.vector.tensor_copy(out=ksg[a][:], in_=ks[:, a * V : (a + 1) * V].indirect(list3[:]))
+
+        for n in range(3):
+            gaps(n)
+        pick_words(0)
+        pick_scales(0)
+        pick_scales(1)
+        gaps(3)
+        pick_words(1)
+        for h in range(HALVES):
+            product(0, h)
+        gaps(4)
+        for c in range(2):
+            nc.tensor.transpose(bps[:, c, :], bcol[:, c : c + 1].to_broadcast([P, P]), ident[:])
+        nc.scalar.copy(out=bias[:].rearrange("p (n c) -> p n c", c=2), in_=bps[:].rearrange("p c n -> p n c"))
+        for n in range(5, 8):
+            gaps(n)
+        for h in range(HALVES):
+            product(1, h)
+
+        score = [sb.tile([P, I], F32, name="score%d" % h) for h in range(HALVES)]
+        best = [sb.tile([P, G], F32, name="best%d" % h) for h in range(HALVES)]
+        top = [sb.tile([P, 1], F32, name="top%d" % h) for h in range(HALVES)]
+        res = sb.tile([P, HALVES, G], F32, name="res")
+        for h in range(HALVES):
+            nc.vector.tensor_tensor(out=score[h][:], in0=acc[h][:], in1=bias[:], op=ALU.add)
+        for h in range(HALVES):
+            nc.vector.tensor_reduce(out=best[h][:], in_=score[h][:].rearrange("p (g b) -> p g b", b=BUNDLE), axis=AX, op=ALU.max)
+        for h in range(HALVES):
+            nc.vector.tensor_reduce(out=top[h][:], in_=best[h][:], axis=AX, op=ALU.max)
+        for h in range(HALVES):
+            nc.vector.scalar_tensor_tensor(out=res[:, h, :], in0=top[h][:].to_broadcast([P, G]), scalar=-0.5,
+                                           in1=best[h][:], op0=ALU.mult, op1=ALU.add)
+        nc.sync.dma_start(out=out.rearrange("(h p) g -> p h g", h=HALVES), in_=res[:])

@@ -49,31 +49,41 @@ def tile_list_scores_gaps_listed_bundles_kernel(tc, xf, fk, ky_words, ky_scales,
         def load_words(a):
             nc.sync.dma_start(out=kw[a][:].bitcast(I32), in_=ky_words[a].bitcast(I32))
 
-        nc.vector.memset(ks[:].bitcast(I32), 0)
         ksr = ky_scales.bitcast(I32).rearrange("a (q r) v -> r q a v", r=4)
+
+        def load_scales(r):
+            nc.sync.dma_start(out=ks[r:P:32, :].bitcast(I32).rearrange("q (a v) -> q a v", a=PASSES), in_=ksr[r])
+
+        warm = sb.tile([P, 2], F32, name="warm")
+        nc.vector.memset(warm[:, 0:1], 0.0)
+        nc.scalar.activation(out=warm[:, 1:2], in_=warm[:, 0:1], func=COPY)
+        nc.gpsimd.memset(ks[:].bitcast(I32), 0)
         make_identity(nc, ident[:])
 
+        nc.sync.dma_start(out=list3[:], in_=offs3)
+        load_words(0)
+        load_words(1)
         load_rows(0)
         nc.sync.dma_start(out=list2[:], in_=offs2)
         nc.sync.dma_start(out=list1[:], in_=offs)
         load_rows(1)
-        nc.sync.dma_start(out=fac[:], in_=fk.rearrange("(a p t) o -> p a (t o)", a=PASSES, t=PACK))
-        nc.sync.dma_start(out=list3[:], in_=offs3)
         load_rows(2)
-        load_words(0)
-        for r in range(4):
-            nc.sync.dma_start(out=ks[r:P:32, :].bitcast(I32).rearrange("q (a v) -> q a v", a=PASSES), in_=ksr[r])
+        nc.sync.dma_start(out=fac[:], in_=fk.rearrange("(a p t) o -> p a (t o)", a=PASSES, t=PACK))
+        load_scales(0)
+        load_scales(1)
+        load_scales(2)
+        load_scales(3)
         load_rows(3)
-        load_words(1)
         load_rows(4)
+        load_rows(5)
+        load_rows(6)
+        load_rows(7)
         nc.sync.dma_start(out=bcol[:], in_=bi.rearrange("o (p c) -> p (o c)", c=2))
-        for n in range(5, 8):
-            load_rows(n)
 
         second = [sb.tile([P, J], F32, name="second%d" % n) for n in range(8)]
-        first = [sb.tile([P, P], F32, name="first%d" % n) for n in range(8)]
-        gap = [[sb.tile([P, P], F32, name="gap%d_%d" % (n, h)) for h in range(HALVES)] for n in range(8)]
-        u = [[sb.tile([P, P * PACK], BF16, name="u%d_%d" % (a, h), align_bytes=64) for h in range(HALVES)] for a in range(PASSES)]
+        first = [sb.tile([P, J], F32, name="first%d" % n) for n in range(8)]
+        gap = [sb.tile([P, PACK * J], F32, name="gap%d" % a) for a in range(PASSES)]
+        u = [sb.tile([P, J * PACK], BF16, name="u%d" % a, align_bytes=64) for a in range(PASSES)]
         uc = [[sb.tile([P, P], U32, name="uc%d_%d" % (a, h), align_bytes=64) for h in range(HALVES)] for a in range(PASSES)]
         us = [[sb.tile([P, P], U8, name="us%d_%d" % (a, h), align_bytes=64) for h in range(HALVES)] for a in range(PASSES)]
         kwg = [sb.tile([P, I], U16, name="kwg%d" % a, align_bytes=64) for a in range(PASSES)]
@@ -81,33 +91,49 @@ def tile_list_scores_gaps_listed_bundles_kernel(tc, xf, fk, ky_words, ky_scales,
         acc = [ps.tile([P, I], F32, name="acc%d" % h) for h in range(HALVES)]
         bps = ps.tile([P, 2, P], F32, name="bps")
 
-        def half(h):
-            return slice(h * P, (h + 1) * P)
+        def entries(lst, lo, hi):
+            return lst[:, lo // 16 : hi // 16]
 
-        def entries(lst, h):
-            return lst[:, 8 * h : 8 * h + 8]
+        def pick(dst, n, lst, lo, hi):
+            nc.scalar.activation(out=dst[n][:, lo:hi], in_=rows[n][:].indirect(entries(lst, lo, hi)), func=COPY)
 
-        def weave(n, h):
+        def gap_of(n, lo, hi):
             a, t = divmod(n, PACK)
-            nc.vector.tensor_scalar(
-                out=u[a][h][:].rearrange("p (j t) -> p j t", t=PACK)[:, :, t],
-                in0=gap[n][h][:], scalar1=fac[:, a, t : t + 1], scalar2=None, op0=ALU.mult)
+            return gap[a][:, t * J + lo : t * J + hi]
+
+        def fused(n, lo, hi):
+            nc.vector.tensor_tensor(out=gap_of(n, lo, hi), in0=rows[n][:].indirect(entries(list1, lo, hi)),
+                                    in1=second[n][:, lo:hi], op=ALU.subtract)
+
+        def sub(n, lo, hi):
+            nc.vector.tensor_tensor(out=gap_of(n, lo, hi), in0=first[n][:, lo:hi], in1=second[n][:, lo:hi], op=ALU.subtract)
+
+        def weave(a, lo, hi):
+            nc.vector.tensor_tensor(
+                out=u[a][:, lo * PACK : hi * PACK].rearrange("p (c i t) -> p c t i", i=4, t=PACK),
+                in0=gap[a][:].rearrange("p (t j) -> p t j", t=PACK)[:, :, lo:hi].rearrange("p t (c i) -> p c t i", i=4),
+                in1=fac[:, a, :].unsqueeze(1).unsqueeze(3).to_broadcast([P, (hi - lo) // 4, PACK, 4]), op=ALU.mult)
 
         def product(a, h):
-            nc.vector.quantize_mx(out=uc[a][h][:].bitcast(E5M2X4), scales=us[a][h][:], in_=u[a][h][:])
+            nc.vector.quantize_mx(out=uc[a][h][:].bitcast(E5M2X4), scales=us[a][h][:],
+                                  in_=u[a][:, h * P * PACK : (h + 1) * P * PACK])
             nc.tensor.matmul_mx(
                 out=acc[h][:], lhsT=uc[a][h][:].bitcast(E5M2X4), lhsT_scale=us[a][h][:],
                 rhs=kwg[a][:].bitcast(E2M1X4), rhs_scale=ksg[a][:], start=(a == 0), stop=(a == PASSES - 1))
 
-        def gaps(n):
-            nc.scalar.activation(out=second[n][:, half(0)], in_=rows[n][:].indirect(entries(list2, 0)), func=COPY)
-            nc.scalar.activation(out=second[n][:, half(1)], in_=rows[n][:].indirect(entries(list2, 1)), func=COPY)
-            nc.scalar.activation(out=first[n][:], in_=rows[n][:].indirect(entries(list1, 1)), func=COPY)
-            nc.vector.tensor_tensor(out=gap[n][0][:], in0=rows[n][:].indirect(entries(list1, 0)),
-                                    in1=second[n][:, half(0)], op=ALU.subtract)
-            weave(n, 0)
-            nc.vector.tensor_tensor(out=gap[n][1][:], in0=first[n][:], in1=second[n][:, half(1)], op=ALU.subtract)
-            weave(n, 1)
+        def gaps(n, split):
+            pick(second, n, list2, 0, J)
+            if split < J:
+                pick(first, n, list1, split, J)
+            if split > 0:
+                fused(n, 0, split)
+            if split < J:
+                sub(n, split, J)
+
+        def spread_bias():
+            for c in range(2):
+                nc.tensor.transpose(bps[:, c, :], bcol[:, c : c + 1].to_broadcast([P, P]), ident[:])
+            nc.scalar.copy(out=bias[:].rearrange("p (n c) -> p n c", c=2), in_=bps[:].rearrange("p c n -> p n c"))
 
         def pick_words(a):
             nc.vector.tensor_copy(out=kwg[a][:], in_=kw[a][:].indirect(list3[:]))
@@ -115,23 +141,31 @@ def tile_list_scores_gaps_listed_bundles_kernel(tc, xf, fk, ky_words, ky_scales,
         def pick_scales(a):
             nc.vector.tensor_copy(out=ksg[a][:], in_=ks[:, a * V : (a + 1) * V].indirect(list3[:]))
 
-        for n in range(3):
-            gaps(n)
+
         pick_words(0)
+        pick_words(1)
+        gaps(0, J)
+        gaps(1, J)
         pick_scales(0)
         pick_scales(1)
-        gaps(3)
-        pick_words(1)
-        for h in range(HALVES):
-            product(0, h)
-        gaps(4)
-        for c in range(2):
-            nc.tensor.transpose(bps[:, c, :], bcol[:, c : c + 1].to_broadcast([P, P]), ident[:])
-        nc.scalar.copy(out=bias[:].rearrange("p (n c) -> p n c", c=2), in_=bps[:].rearrange("p c n -> p n c"))
-        for n in range(5, 8):
-            gaps(n)
-        for h in range(HALVES):
-            product(1, h)
+        gaps(2, 0)
+        gaps(3, J)
+        weave(0, 0, J)
+        product(0, 0)
+        product(0, 1)
+        gaps(4, 0)
+        gaps(5, 0)
+        gaps(6, J)
+        pick(second, 7, list2, 0, P)
+        pick(second, 7, list2, P, J)
+        pick(first, 7, list1, P, J)
+        fused(7, 0, P)
+        spread_bias()
+        weave(1, 0, P)
+        sub(7, P, J)
+        product(1, 0)
+        weave(1, P, J)
+        product(1, 1)
 
         score = [sb.tile([P, I], F32, name="score%d" % h) for h in range(HALVES)]
         best = [sb.tile([P, G], F32, name="best%d" % h) for h in range(HALVES)]

from contextlib import ExitStack

import concourse.mybir as mybir
from concourse.masks import make_identity

K, T, J, I, V, G = 1024, 1024, 256, 256, 1024, 32
FLOPS = 2 * K * J * I

F32 = mybir.dt.float32
BF16 = mybir.dt.bfloat16
I32 = mybir.dt.int32
U32 = mybir.dt.uint32
U16 = mybir.dt.uint16
U8 = mybir.dt.uint8
E5M2X4 = mybir.dt.float8_e5m2_x4
E2M1X4 = mybir.dt.float4_e2m1fn_x4
ALU = mybir.AluOpType
COPY = mybir.ActivationFunctionType.Copy
AX = mybir.AxisListType.X

P = 128
PACK = 4
PASSES = K // (P * PACK)
HALVES = J // P
BUNDLE = I // G


def tile_list_scores_gaps_listed_bundles_kernel(tc, xf, fk, ky_words, ky_scales, bi, offs, offs2, offs3, out):
    nc = tc.nc
    with ExitStack() as ctx:
        sb = ctx.enter_context(tc.tile_pool(name="sb", bufs=1))
        ps = ctx.enter_context(tc.psum_pool(name="ps", bufs=1))

        list1 = sb.tile([P, J // 16], U16, name="list1")
        list2 = sb.tile([P, J // 16], U16, name="list2")
        list3 = sb.tile([P, I // 16], U16, name="list3")
        rows = [sb.tile([P, T], F32, name="rows%d" % n) for n in range(8)]
        kw = [sb.tile([P, V], U16, name="kw%d" % a) for a in range(PASSES)]
        ks = sb.tile([P, PASSES * V], U8, name="ks")
        fac = sb.tile([P, PASSES, PACK], F32, name="fac")
        bcol = sb.tile([P, 2], F32, name="bcol")
        ident = sb.tile([P, P], F32, name="ident")
        bias = sb.tile([P, I], F32, name="bias")
        xr = xf.rearrange("(a p t) c -> a t p c", a=PASSES, t=PACK)

        def load_rows(n):
            nc.sync.dma_start(out=rows[n][:], in_=xr[n // PACK, n % PACK])

        def load_words(a):
            nc.sync.dma_start(out=kw[a][:].bitcast(I32), in_=ky_words[a].bitcast(I32))

        ksr = ky_scales.bitcast(I32).rearrange("a (q r) v -> r q a v", r=4)

        def load_scales(r):
            nc.sync.dma_start(out=ks[r:P:32, :].bitcast(I32).rearrange("q (a v) -> q a v", a=PASSES), in_=ksr[r])

        warm = sb.tile([P, 2], F32, name="warm")
        nc.vector.memset(warm[:, 0:1], 0.0)
        nc.scalar.activation(out=warm[:, 1:2], in_=warm[:, 0:1], func=COPY)
        nc.gpsimd.memset(ks[:].bitcast(I32), 0)
        make_identity(nc, ident[:])

        nc.sync.dma_start(out=list3[:], in_=offs3)
        load_words(0)
        load_words(1)
        load_rows(0)
        nc.sync.dma_start(out=list2[:], in_=offs2)
        nc.sync.dma_start(out=list1[:], in_=offs)
        load_rows(1)
        load_rows(2)
        nc.sync.dma_start(out=fac[:], in_=fk.rearrange("(a p t) o -> p a (t o)", a=PASSES, t=PACK))
        load_scales(0)
        load_scales(1)
        load_scales(2)
        load_scales(3)
        load_rows(3)
        load_rows(4)
        load_rows(5)
        load_rows(6)
        load_rows(7)
        nc.sync.dma_start(out=bcol[:], in_=bi.rearrange("o (p c) -> p (o c)", c=2))

        second = [sb.tile([P, J], F32, name="second%d" % n) for n in range(8)]
        first = [sb.tile([P, J], F32, name="first%d" % n) for n in range(8)]
        gap = [sb.tile([P, PACK * J], F32, name="gap%d" % a) for a in range(PASSES)]
        u = [sb.tile([P, J * PACK], BF16, name="u%d" % a, align_bytes=64) for a in range(PASSES)]
        uc = [[sb.tile([P, P], U32, name="uc%d_%d" % (a, h), align_bytes=64) for h in range(HALVES)] for a in range(PASSES)]
        us = [[sb.tile([P, P], U8, name="us%d_%d" % (a, h), align_bytes=64) for h in range(HALVES)] for a in range(PASSES)]
        kwg = [sb.tile([P, I], U16, name="kwg%d" % a, align_bytes=64) for a in range(PASSES)]
        ksg = [sb.tile([P, I], U8, name="ksg%d" % a, align_bytes=64) for a in range(PASSES)]
        acc = [ps.tile([P, I], F32, name="acc%d" % h) for h in range(HALVES)]
        bps = ps.tile([P, 2, P], F32, name="bps")

        def entries(lst, lo, hi):
            return lst[:, lo // 16 : hi // 16]

        def pick(dst, n, lst, lo, hi):
            nc.scalar.activation(out=dst[n][:, lo:hi], in_=rows[n][:].indirect(entries(lst, lo, hi)), func=COPY)

        def gap_of(n, lo, hi):
            a, t = divmod(n, PACK)
            return gap[a][:, t * J + lo : t * J + hi]

        def fused(n, lo, hi):
            nc.vector.tensor_tensor(out=gap_of(n, lo, hi), in0=rows[n][:].indirect(entries(list1, lo, hi)),
                                    in1=second[n][:, lo:hi], op=ALU.subtract)

        def sub(n, lo, hi):
            nc.vector.tensor_tensor(out=gap_of(n, lo, hi), in0=first[n][:, lo:hi], in1=second[n][:, lo:hi], op=ALU.subtract)

        def weave(a, lo, hi):
            nc.vector.tensor_tensor(
                out=u[a][:, lo * PACK : hi * PACK].rearrange("p (c i t) -> p c t i", i=4, t=PACK),
                in0=gap[a][:].rearrange("p (t j) -> p t j", t=PACK)[:, :, lo:hi].rearrange("p t (c i) -> p c t i", i=4),
                in1=fac[:, a, :].unsqueeze(1).unsqueeze(3).to_broadcast([P, (hi - lo) // 4, PACK, 4]), op=ALU.mult)

        def product(a, h):
            nc.vector.quantize_mx(out=uc[a][h][:].bitcast(E5M2X4), scales=us[a][h][:],
                                  in_=u[a][:, h * P * PACK : (h + 1) * P * PACK])
            nc.tensor.matmul_mx(
                out=acc[h][:], lhsT=uc[a][h][:].bitcast(E5M2X4), lhsT_scale=us[a][h][:],
                rhs=kwg[a][:].bitcast(E2M1X4), rhs_scale=ksg[a][:], start=(a == 0), stop=(a == PASSES - 1))

        def gaps(n, split):
            pick(second, n, list2, 0, J)
            if split < J:
                pick(first, n, list1, split, J)
            if split > 0:
                fused(n, 0, split)
            if split < J:
                sub(n, split, J)

        def spread_bias():
            for c in range(2):
                nc.tensor.transpose(bps[:, c, :], bcol[:, c : c + 1].to_broadcast([P, P]), ident[:])
            nc.scalar.copy(out=bias[:].rearrange("p (n c) -> p n c", c=2), in_=bps[:].rearrange("p c n -> p n c"))

        def pick_words(a):
            nc.vector.tensor_copy(out=kwg[a][:], in_=kw[a][:].indirect(list3[:]))

        def pick_scales(a):
            nc.vector.tensor_copy(out=ksg[a][:], in_=ks[:, a * V : (a + 1) * V].indirect(list3[:]))


        pick_words(0)
        pick_words(1)
        gaps(0, J)
        gaps(1, J)
        pick_scales(0)
        pick_scales(1)
        gaps(2, 0)
        gaps(3, J)
        weave(0, 0, J)
        product(0, 0)
        product(0, 1)
        gaps(4, 0)
        gaps(5, 0)
        gaps(6, J)
        pick(second, 7, list2, 0, P)
        pick(second, 7, list2, P, J)
        pick(first, 7, list1, P, J)
        fused(7, 0, P)
        spread_bias()
        weave(1, 0, P)
        sub(7, P, J)
        product(1, 0)
        weave(1, P, J)
        product(1, 1)

        score = [sb.tile([P, I], F32, name="score%d" % h) for h in range(HALVES)]
        best = [sb.tile([P, G], F32, name="best%d" % h) for h in range(HALVES)]
        top = [sb.tile([P, 1], F32, name="top%d" % h) for h in range(HALVES)]
        res = sb.tile([P, HALVES, G], F32, name="res")
        for h in range(HALVES):
            nc.vector.tensor_tensor(out=score[h][:], in0=acc[h][:], in1=bias[:], op=ALU.add)
        for h in range(HALVES):
            nc.vector.tensor_reduce(out=best[h][:], in_=score[h][:].rearrange("p (g b) -> p g b", b=BUNDLE), axis=AX, op=ALU.max)
        for h in range(HALVES):
            nc.vector.tensor_reduce(out=top[h][:], in_=best[h][:], axis=AX, op=ALU.max)
        for h in range(HALVES):
            nc.vector.scalar_tensor_tensor(out=res[:, h, :], in0=top[h][:].to_broadcast([P, G]), scalar=-0.5,
                                           in1=best[h][:], op0=ALU.mult, op1=ALU.add)
        nc.sync.dma_start(out=out.rearrange("(h p) g -> p h g", h=HALVES), in_=res[:])
